import numpy as np, ml_dtypes
CORES = [30,158,46,174,86,214]
N = 6
K, F = 2, 64
def setup_inputs(rng):
    return {"gr": rng.standard_normal((N, K, 128, N * F), dtype=np.float32).astype(ml_dtypes.bfloat16)}
def setup_inputs_big(rng):
    d = setup_inputs(rng)
    for k in ("gr",): d[k] = (d[k].astype(np.float32) * 1048576.0).astype(d[k].dtype)
    return d
def setup_inputs_small(rng):
    d = setup_inputs(rng)
    for k in ("gr",): d[k] = (d[k].astype(np.float32) * (1 / 1048576.0)).astype(d[k].dtype)
    return d
def reference(gr):
    s = gr.astype(np.float64).sum(axis=(0, 1))
    return {"y": np.stack([s[:, F * r:F * r + F] for r in range(N)]).astype(np.float32 if gr.dtype != np.float64 else np.float64)}

@@ -1,0 +1,103 @@
+from concourse.bass import DstId, RemoteDMATransfer
+from concourse.mybir import AluOpType
+
+N, K, F = 6, 2, 64
+
+SCRATCH = {
+    "st0": ("sbuf", [128, N * F], "bfloat16"),
+    "st1": ("sbuf", [128, N * F], "bfloat16"),
+    "sumf": ("sbuf", [128, N * F], "float32"),
+    "land": ("sbuf", [128, (N - 1) * F], "float32"),
+    "t": ("sbuf", [128, 2 * F], "float32"),
+    "u": ("sbuf", [128, F], "float32"),
+    "w": ("sbuf", [128, F], "float32"),
+    "out": ("sbuf", [128, F], "float32"),
+}
+SEMAPHORES = ["ld", "pre1", "pre2", "preo", "arr1", "arr2", "sent", "va", "vb", "vc", "fin", "stored"]
+
+
+def _engines(m):
+    return [1 << b for b in range(m.bit_length()) if (m >> b) & 1]
+
+
+def _plan(cores, topo):
+    n = len(cores)
+    late, early = [], []
+    for s in range(n):
+        twin = [q for q in range(n) if q != s and topo.same_plane(cores[s], cores[q]) and topo.chip(cores[q]) == topo.chip(cores[s])]
+        late.append(twin[0])
+    for s in range(n):
+        ds = [(s + o) % n for o in range(1, n) if (s + o) % n != late[s]]
+        common = topo.mask(cores[s], cores[ds[0]])
+        for d in ds:
+            common &= topo.mask(cores[s], cores[d])
+        eng = _engines(common)
+        per = 1
+        while per * 2 * len(ds) <= len(eng):
+            per *= 2
+        early.append({d: sum(eng[i * per:(i + 1) * per]) for i, d in enumerate(ds)})
+    return late, early
+
+
+def rank_program(g, core, T, topo):
+    r = T.rank_of(core)
+    if r is None:
+        return
+    cores = list(T.cores)
+    n = len(cores)
+    late, early = _plan(cores, topo)
+    sem, v, add = T.sem, g.vector, AluOpType.add
+
+    def early_sources(d):
+        return [s for s in range(n) if d in early[s]]
+
+    def count(m):
+        return len(_engines(m))
+
+    g.sync.dma_start(T.st0[:], T.gr[0]).then_inc(sem.ld, 16)
+    g.scalar.dma_start(T.st1[:], T.gr[1]).then_inc(sem.ld, 16)
+
+    first = sorted(early[r])
+    runs = []
+    for d in first:
+        if runs and runs[-1][1] == d:
+            runs[-1][1] = d + 1
+        else:
+            runs.append([d, d + 1])
+    v.wait_ge(sem.ld, 32)
+    for a, b in runs:
+        v.tensor_tensor(T.sumf[:, a * F:b * F], T.st0[:, a * F:b * F], T.st1[:, a * F:b * F], add).then_inc(sem.pre1, 1)
+    for d, s_ in ((late[r], sem.pre2), (r, sem.preo)):
+        v.tensor_tensor(T.sumf[:, d * F:(d + 1) * F], T.st0[:, d * F:(d + 1) * F], T.st1[:, d * F:(d + 1) * F], add).then_inc(s_, 1)
+
+    trs = []
+    for d, m in early[r].items():
+        rid, pid = topo.addr(cores[d], core)
+        slot = early_sources(d).index(r)
+        trs.append(RemoteDMATransfer(dst_ids=[DstId(rid=rid, pnc=pid)], dma_engine_mask=m, remote_sem=sem.arr1,
+                                     src=T.sumf[:, d * F:(d + 1) * F], dst=T.land[:, slot * F:(slot + 1) * F]))
+    g.wait_ge(sem.pre1, len(runs))
+    g.remote_dma_fused(trs, local_sem=sem.sent)
+    d = late[r]
+    rid, pid = topo.addr(cores[d], core)
+    lm = topo.mask(core, cores[d])
+    g.wait_ge(sem.pre2, 1)
+    g.remote_dma(out_ap=T.land[:, (n - 2) * F:(n - 1) * F], in_ap=T.sumf[:, d * F:(d + 1) * F], remote_sem=sem.arr2,
+                 local_sem=sem.sent, pid=pid, routing_id=rid, dma_engine_mask=lm)
+
+    v.wait_ge(sem.arr1, sum(count(early[s][r]) for s in early_sources(r)))
+    v.tensor_tensor(T.t[:], T.land[:, 0:2 * F], T.land[:, 2 * F:4 * F], add).then_inc(sem.va, 1)
+    v.wait_ge(sem.va, 1)
+    v.tensor_tensor(T.u[:], T.t[:, 0:F], T.t[:, F:2 * F], add).then_inc(sem.vb, 1)
+    v.wait_ge(sem.vb, 1)
+    v.wait_ge(sem.preo, 1)
+    v.tensor_tensor(T.w[:], T.u[:], T.sumf[:, r * F:(r + 1) * F], add).then_inc(sem.vc, 1)
+    v.wait_ge(sem.vc, 1)
+    src = late.index(r)
+    v.wait_ge(sem.arr2, count(topo.mask(cores[src], core)))
+    v.tensor_tensor(T.out[:], T.w[:], T.land[:, (n - 2) * F:(n - 1) * F], add).then_inc(sem.fin, 1)
+
+    g.sync.wait_ge(sem.fin, 1)
+    g.sync.dma_start(T.y[:], T.out[:]).then_inc(sem.stored, 16)
+    g.sync.wait_ge(sem.stored, 16)
+    g.wait_ge(sem.sent, sum(count(m) for m in early[r].values()) + count(lm))

@@ -2,41 +2,36 @@ from concourse.bass import DstId, RemoteDMATransfer
 from concourse.mybir import AluOpType
 
 N, K, F = 6, 2, 64
+H = N // 2
 
 SCRATCH = {
     "st0": ("sbuf", [128, N * F], "bfloat16"),
     "st1": ("sbuf", [128, N * F], "bfloat16"),
     "sumf": ("sbuf", [128, N * F], "float32"),
-    "land": ("sbuf", [128, (N - 1) * F], "float32"),
-    "t": ("sbuf", [128, 2 * F], "float32"),
-    "u": ("sbuf", [128, F], "float32"),
-    "w": ("sbuf", [128, F], "float32"),
+    "raw": ("sbuf", [128, K * F], "bfloat16"),
+    "land": ("sbuf", [128, 4 * F], "float32"),
+    "rs": ("sbuf", [128, F], "float32"),
     "out": ("sbuf", [128, F], "float32"),
+    "pa": ("psum", [128, F], "float32"),
+    "pb": ("psum", [128, F], "float32"),
 }
-SEMAPHORES = ["ld", "pre1", "pre2", "preo", "arr1", "arr2", "sent", "va", "vb", "vc", "fin", "stored"]
+SEMAPHORES = ["ld1", "ld2", "pre1", "pre2", "arr0", "arr1", "arr2a", "arr2b", "sent", "vs", "fin", "stored"]
 
 
 def _engines(m):
     return [1 << b for b in range(m.bit_length()) if (m >> b) & 1]
 
 
-def _plan(cores, topo):
-    n = len(cores)
-    late, early = [], []
-    for s in range(n):
-        twin = [q for q in range(n) if q != s and topo.same_plane(cores[s], cores[q]) and topo.chip(cores[q]) == topo.chip(cores[s])]
-        late.append(twin[0])
-    for s in range(n):
-        ds = [(s + o) % n for o in range(1, n) if (s + o) % n != late[s]]
-        common = topo.mask(cores[s], cores[ds[0]])
-        for d in ds:
-            common &= topo.mask(cores[s], cores[d])
-        eng = _engines(common)
-        per = 1
-        while per * 2 * len(ds) <= len(eng):
-            per *= 2
-        early.append({d: sum(eng[i * per:(i + 1) * per]) for i, d in enumerate(ds)})
-    return late, early
+def _halves(m):
+    e = _engines(m)
+    return sum(e[:len(e) // 2]), sum(e[len(e) // 2:])
+
+
+def _sched(s):
+    far = [d for d in range(N) if d // H != s // H]
+    near = [d for d in range(N) if d // H == s // H and d != s]
+    first = (s + H) % N
+    return first, [d for d in far if d != first], near
 
 
 def rank_program(g, core, T, topo):
@@ -44,60 +39,90 @@ def rank_program(g, core, T, topo):
     if r is None:
         return
     cores = list(T.cores)
-    n = len(cores)
-    late, early = _plan(cores, topo)
     sem, v, add = T.sem, g.vector, AluOpType.add
+    first, mid, last = _sched(r)
 
-    def early_sources(d):
-        return [s for s in range(n) if d in early[s]]
+    def blk(d):
+        return slice(d * F, (d + 1) * F)
+
+    def late_sources(d):
+        ss = [s for s in range(N) if d in _sched(s)[2]]
+        return sorted(ss, key=lambda s: (not topo.same_plane(cores[s], cores[d]), s))
+
+    def mid_sources(d):
+        return [s for s in range(N) if d in _sched(s)[1]]
+
+    def pair_masks(ds):
+        m = topo.mask(core, cores[ds[0]])
+        for d in ds:
+            m &= topo.mask(core, cores[d])
+        return _halves(m)
+
+    def transfer(d, m, rsem, src, dst):
+        rid, pid = topo.addr(cores[d], core)
+        return RemoteDMATransfer(dst_ids=[DstId(rid=rid, pnc=pid)], dma_engine_mask=m, remote_sem=rsem, src=src, dst=dst)
 
     def count(m):
         return len(_engines(m))
 
-    g.sync.dma_start(T.st0[:], T.gr[0]).then_inc(sem.ld, 16)
-    g.scalar.dma_start(T.st1[:], T.gr[1]).then_inc(sem.ld, 16)
+    fa, na = (first // H) * H * F, (r // H) * H * F
+    far, near = slice(fa, fa + H * F), slice(na, na + H * F)
+    g.sync.dma_start(T.st0[:, far], T.gr[0, :, far]).then_inc(sem.ld1, 16)
+    g.scalar.dma_start(T.st1[:, far], T.gr[1, :, far]).then_inc(sem.ld1, 16)
+    g.sync.dma_start(T.st0[:, near], T.gr[0, :, near]).then_inc(sem.ld2, 16)
+    g.scalar.dma_start(T.st1[:, near], T.gr[1, :, near]).then_inc(sem.ld2, 16)
 
-    first = sorted(early[r])
-    runs = []
-    for d in first:
-        if runs and runs[-1][1] == d:
-            runs[-1][1] = d + 1
-        else:
-            runs.append([d, d + 1])
-    v.wait_ge(sem.ld, 32)
-    for a, b in runs:
-        v.tensor_tensor(T.sumf[:, a * F:b * F], T.st0[:, a * F:b * F], T.st1[:, a * F:b * F], add).then_inc(sem.pre1, 1)
-    for d, s_ in ((late[r], sem.pre2), (r, sem.preo)):
-        v.tensor_tensor(T.sumf[:, d * F:(d + 1) * F], T.st0[:, d * F:(d + 1) * F], T.st1[:, d * F:(d + 1) * F], add).then_inc(s_, 1)
+    sent = 0
+    ma, mb = pair_masks([first])
+    g.wait_ge(sem.ld1, 32)
+    g.remote_dma_fused([transfer(first, ma, sem.arr0, T.st0[:, blk(first)], T.raw[:, 0:F]),
+                        transfer(first, mb, sem.arr0, T.st1[:, blk(first)], T.raw[:, F:2 * F])], local_sem=sem.sent)
+    sent += count(ma) + count(mb)
 
+    v.wait_ge(sem.ld1, 32)
+    for d in mid:
+        v.tensor_tensor(T.sumf[:, blk(d)], T.st0[:, blk(d)], T.st1[:, blk(d)], add).then_inc(sem.pre1, 1)
+    v.wait_ge(sem.ld2, 32)
+    for d in last:
+        v.tensor_tensor(T.sumf[:, blk(d)], T.st0[:, blk(d)], T.st1[:, blk(d)], add).then_inc(sem.pre2, 1)
+    v.tensor_tensor(T.pa[:], T.st0[:, blk(r)], T.st1[:, blk(r)], add).then_inc(sem.vs, 1)
+
+    ms = pair_masks(mid)
+    g.wait_ge(sem.pre1, len(mid))
+    g.remote_dma_fused([transfer(d, m, sem.arr1, T.sumf[:, blk(d)], T.land[:, blk(mid_sources(d).index(r))])
+                        for d, m in zip(mid, ms)], local_sem=sem.sent)
+    sent += sum(count(m) for m in ms)
+    ml = pair_masks(last)
+    g.wait_ge(sem.pre2, len(last))
     trs = []
-    for d, m in early[r].items():
-        rid, pid = topo.addr(cores[d], core)
-        slot = early_sources(d).index(r)
-        trs.append(RemoteDMATransfer(dst_ids=[DstId(rid=rid, pnc=pid)], dma_engine_mask=m, remote_sem=sem.arr1,
-                                     src=T.sumf[:, d * F:(d + 1) * F], dst=T.land[:, slot * F:(slot + 1) * F]))
-    g.wait_ge(sem.pre1, len(runs))
+    for d, m in zip(last, ml):
+        j = late_sources(d).index(r)
+        trs.append(transfer(d, m, (sem.arr2a, sem.arr2b)[j], T.sumf[:, blk(d)], T.land[:, blk(2 + j)]))
     g.remote_dma_fused(trs, local_sem=sem.sent)
-    d = late[r]
-    rid, pid = topo.addr(cores[d], core)
-    lm = topo.mask(core, cores[d])
-    g.wait_ge(sem.pre2, 1)
-    g.remote_dma(out_ap=T.land[:, (n - 2) * F:(n - 1) * F], in_ap=T.sumf[:, d * F:(d + 1) * F], remote_sem=sem.arr2,
-                 local_sem=sem.sent, pid=pid, routing_id=rid, dma_engine_mask=lm)
+    sent += sum(count(m) for m in ml)
 
-    v.wait_ge(sem.arr1, sum(count(early[s][r]) for s in early_sources(r)))
-    v.tensor_tensor(T.t[:], T.land[:, 0:2 * F], T.land[:, 2 * F:4 * F], add).then_inc(sem.va, 1)
-    v.wait_ge(sem.va, 1)
-    v.tensor_tensor(T.u[:], T.t[:, 0:F], T.t[:, F:2 * F], add).then_inc(sem.vb, 1)
-    v.wait_ge(sem.vb, 1)
-    v.wait_ge(sem.preo, 1)
-    v.tensor_tensor(T.w[:], T.u[:], T.sumf[:, r * F:(r + 1) * F], add).then_inc(sem.vc, 1)
-    v.wait_ge(sem.vc, 1)
-    src = late.index(r)
-    v.wait_ge(sem.arr2, count(topo.mask(cores[src], core)))
-    v.tensor_tensor(T.out[:], T.w[:], T.land[:, (n - 2) * F:(n - 1) * F], add).then_inc(sem.fin, 1)
+    def half(s):
+        return count(_halves(topo.mask(cores[s], core))[0])
+
+    src0 = [s for s in range(N) if _sched(s)[0] == r][0]
+    v.wait_ge(sem.arr0, 2 * half(src0))
+    v.tensor_tensor(T.rs[:], T.raw[:, 0:F], T.raw[:, F:2 * F], add).then_inc(sem.vs, 1)
+    v.wait_ge(sem.vs, 2)
+    v.tensor_tensor(T.pb[:], T.pa[:], T.rs[:], add).then_inc(sem.vs, 1)
+    v.wait_ge(sem.vs, 3)
+    v.wait_ge(sem.arr1, sum(half(s) for s in mid_sources(r)))
+    v.tensor_tensor(T.pa[:], T.pb[:], T.land[:, blk(0)], add).then_inc(sem.vs, 1)
+    v.wait_ge(sem.vs, 4)
+    v.tensor_tensor(T.pb[:], T.pa[:], T.land[:, blk(1)], add).then_inc(sem.vs, 1)
+    v.wait_ge(sem.vs, 5)
+    la, lb = late_sources(r)
+    v.wait_ge(sem.arr2a, half(la))
+    v.tensor_tensor(T.pa[:], T.pb[:], T.land[:, blk(2)], add).then_inc(sem.vs, 1)
+    v.wait_ge(sem.vs, 6)
+    v.wait_ge(sem.arr2b, half(lb))
+    v.tensor_tensor(T.out[:], T.pa[:], T.land[:, blk(3)], add).then_inc(sem.fin, 1)
 
     g.sync.wait_ge(sem.fin, 1)
     g.sync.dma_start(T.y[:], T.out[:]).then_inc(sem.stored, 16)
     g.sync.wait_ge(sem.stored, 16)
-    g.wait_ge(sem.sent, sum(count(m) for m in early[r].values()) + count(lm))
+    g.wait_ge(sem.sent, sent)

from concourse.bass import DstId, RemoteDMATransfer
from concourse.mybir import AluOpType

N, K, F = 6, 2, 64
H = N // 2

SCRATCH = {
    "st0": ("sbuf", [128, N * F], "bfloat16"),
    "st1": ("sbuf", [128, N * F], "bfloat16"),
    "sumf": ("sbuf", [128, N * F], "float32"),
    "raw": ("sbuf", [128, K * F], "bfloat16"),
    "land": ("sbuf", [128, 4 * F], "float32"),
    "rs": ("sbuf", [128, F], "float32"),
    "out": ("sbuf", [128, F], "float32"),
    "pa": ("psum", [128, F], "float32"),
    "pb": ("psum", [128, F], "float32"),
}
SEMAPHORES = ["ld1", "ld2", "pre1", "pre2", "arr0", "arr1", "arr2a", "arr2b", "sent", "vs", "fin", "stored"]


def _engines(m):
    return [1 << b for b in range(m.bit_length()) if (m >> b) & 1]


def _halves(m):
    e = _engines(m)
    return sum(e[:len(e) // 2]), sum(e[len(e) // 2:])


def _sched(s):
    far = [d for d in range(N) if d // H != s // H]
    near = [d for d in range(N) if d // H == s // H and d != s]
    first = (s + H) % N
    return first, [d for d in far if d != first], near


def rank_program(g, core, T, topo):
    r = T.rank_of(core)
    if r is None:
        return
    cores = list(T.cores)
    sem, v, add = T.sem, g.vector, AluOpType.add
    first, mid, last = _sched(r)

    def blk(d):
        return slice(d * F, (d + 1) * F)

    def late_sources(d):
        ss = [s for s in range(N) if d in _sched(s)[2]]
        return sorted(ss, key=lambda s: (not topo.same_plane(cores[s], cores[d]), s))

    def mid_sources(d):
        return [s for s in range(N) if d in _sched(s)[1]]

    def pair_masks(ds):
        m = topo.mask(core, cores[ds[0]])
        for d in ds:
            m &= topo.mask(core, cores[d])
        return _halves(m)

    def transfer(d, m, rsem, src, dst):
        rid, pid = topo.addr(cores[d], core)
        return RemoteDMATransfer(dst_ids=[DstId(rid=rid, pnc=pid)], dma_engine_mask=m, remote_sem=rsem, src=src, dst=dst)

    def count(m):
        return len(_engines(m))

    fa, na = (first // H) * H * F, (r // H) * H * F
    far, near = slice(fa, fa + H * F), slice(na, na + H * F)
    g.sync.dma_start(T.st0[:, far], T.gr[0, :, far]).then_inc(sem.ld1, 16)
    g.scalar.dma_start(T.st1[:, far], T.gr[1, :, far]).then_inc(sem.ld1, 16)
    g.sync.dma_start(T.st0[:, near], T.gr[0, :, near]).then_inc(sem.ld2, 16)
    g.scalar.dma_start(T.st1[:, near], T.gr[1, :, near]).then_inc(sem.ld2, 16)

    sent = 0
    ma, mb = pair_masks([first])
    g.wait_ge(sem.ld1, 32)
    g.remote_dma_fused([transfer(first, ma, sem.arr0, T.st0[:, blk(first)], T.raw[:, 0:F]),
                        transfer(first, mb, sem.arr0, T.st1[:, blk(first)], T.raw[:, F:2 * F])], local_sem=sem.sent)
    sent += count(ma) + count(mb)

    v.wait_ge(sem.ld1, 32)
    for d in mid:
        v.tensor_tensor(T.sumf[:, blk(d)], T.st0[:, blk(d)], T.st1[:, blk(d)], add).then_inc(sem.pre1, 1)
    v.wait_ge(sem.ld2, 32)
    for d in last:
        v.tensor_tensor(T.sumf[:, blk(d)], T.st0[:, blk(d)], T.st1[:, blk(d)], add).then_inc(sem.pre2, 1)
    v.tensor_tensor(T.pa[:], T.st0[:, blk(r)], T.st1[:, blk(r)], add).then_inc(sem.vs, 1)

    ms = pair_masks(mid)
    g.wait_ge(sem.pre1, len(mid))
    g.remote_dma_fused([transfer(d, m, sem.arr1, T.sumf[:, blk(d)], T.land[:, blk(mid_sources(d).index(r))])
                        for d, m in zip(mid, ms)], local_sem=sem.sent)
    sent += sum(count(m) for m in ms)
    ml = pair_masks(last)
    g.wait_ge(sem.pre2, len(last))
    trs = []
    for d, m in zip(last, ml):
        j = late_sources(d).index(r)
        trs.append(transfer(d, m, (sem.arr2a, sem.arr2b)[j], T.sumf[:, blk(d)], T.land[:, blk(2 + j)]))
    g.remote_dma_fused(trs, local_sem=sem.sent)
    sent += sum(count(m) for m in ml)

    def half(s):
        return count(_halves(topo.mask(cores[s], core))[0])

    src0 = [s for s in range(N) if _sched(s)[0] == r][0]
    v.wait_ge(sem.arr0, 2 * half(src0))
    v.tensor_tensor(T.rs[:], T.raw[:, 0:F], T.raw[:, F:2 * F], add).then_inc(sem.vs, 1)
    v.wait_ge(sem.vs, 2)
    v.tensor_tensor(T.pb[:], T.pa[:], T.rs[:], add).then_inc(sem.vs, 1)
    v.wait_ge(sem.vs, 3)
    v.wait_ge(sem.arr1, sum(half(s) for s in mid_sources(r)))
    v.tensor_tensor(T.pa[:], T.pb[:], T.land[:, blk(0)], add).then_inc(sem.vs, 1)
    v.wait_ge(sem.vs, 4)
    v.tensor_tensor(T.pb[:], T.pa[:], T.land[:, blk(1)], add).then_inc(sem.vs, 1)
    v.wait_ge(sem.vs, 5)
    la, lb = late_sources(r)
    v.wait_ge(sem.arr2a, half(la))
    v.tensor_tensor(T.pa[:], T.pb[:], T.land[:, blk(2)], add).then_inc(sem.vs, 1)
    v.wait_ge(sem.vs, 6)
    v.wait_ge(sem.arr2b, half(lb))
    v.tensor_tensor(T.out[:], T.pa[:], T.land[:, blk(3)], add).then_inc(sem.fin, 1)

    g.sync.wait_ge(sem.fin, 1)
    g.sync.dma_start(T.y[:], T.out[:]).then_inc(sem.stored, 16)
    g.sync.wait_ge(sem.stored, 16)
    g.wait_ge(sem.sent, sent)
